import numpy as np, ml_dtypes
CORES = [50,106,114,52,108,116]
N = 6
import mx_ref
NC = 128
LR = np.float32(0.01425)
BF = ml_dtypes.bfloat16
def cut(t, i, w=512):
    return t[:, w * i:w * i + w]
def tile(rs):
    return np.stack(rs, axis=2).reshape(128, -1).astype(BF)
def pick(b):
    s = np.zeros((128, 128, 4), np.float32)
    s[np.arange(128), np.arange(128), b] = 1.0
    return mx_ref.quantize(s.reshape(128, 512).astype(BF))
def setup_inputs(rng):
    def f(*shape):
        return mx_ref.flush((rng.standard_normal(shape, dtype=np.float32) * np.exp2(rng.integers(-2, 3, shape[:-1] + (1,)))).astype(BF))
    return {"b": f(N, 128, N * 512), "w": f(N, 128, 512), "x": f(N, 128, 4 * NC)}
def setup_inputs_blocks(rng):
    d = setup_inputs(rng)
    for k in ("b", "w", "x"): d[k] = mx_ref.spread(d[k], rng, 2)
    return d
def setup_inputs_wide(rng):
    d = setup_inputs(rng)
    for k in ("b", "w", "x"): d[k] = mx_ref.flush((d[k].astype(np.float32) * np.exp2(rng.integers(-4, 5, (N, 1, 1))).astype(np.float32)).astype(BF))
    return d
def reference(b, w, x, own=None):
    S = [pick(t) for t in range(4)]
    h = np.zeros((N, 128, 512), BF)
    for c in range(N):
        for r in range(N):
            q = mx_ref.quantize(cut(b[r], c))
            P = [mx_ref.matmul(S[t], q) for t in range(4)]
            Z = P if r == 0 else [z + p for z, p in zip(Z, P)]
        h[c] = tile([w[c].astype(np.float32)[:, t::4] - Z[t] * LR for t in range(4)])
    use = h if own is None else own["h"]
    H = [mx_ref.quantize(use[j]) for j in range(N)]
    y = np.zeros((N, 128, N * NC), np.float32)
    for r in range(N):
        qx = mx_ref.quantize(x[r])
        for j in range(N):
            y[r][:, NC * j:NC * j + NC] = mx_ref.matmul(H[j], qx)
    return {"h": h, "y": y}

@@ -1,0 +1,252 @@
+import numpy as np
+from concourse.bass import DstId, RemoteDMATransfer
+from concourse.mybir import dt, AluOpType, ActivationFunctionType
+
+N = 6
+W = 128
+CODE = "float8_e4m3fn_x4"
+SCRATCH = {
+    "bt": ("sbuf", [128, N * 512], "bfloat16"),
+    "xt": ("sbuf", [128, 512], "bfloat16"),
+    "wt": ("sbuf", [128, 512], "bfloat16"),
+    "ht": ("sbuf", [128, 512], "bfloat16"),
+    "eye": ("sbuf", [128, 128], "bfloat16"),
+    "pickt": ("sbuf", [128, 516], "bfloat16"),
+    "zc": ("sbuf", [128, 512], "float32"),
+    "yt": ("sbuf", [128, N * W], "float32"),
+    "gq": ("sbuf", [128, N * W], CODE), "gs": ("sbuf", [128, N * W], "uint8"),
+    "sq": ("sbuf", [128, 4 * W], CODE), "ss": ("sbuf", [128, 4 * W], "uint8"),
+    "xq": ("sbuf", [128, W], CODE), "xs": ("sbuf", [128, W], "uint8"),
+    "hq": ("sbuf", [128, W], CODE), "hs": ("sbuf", [128, W], "uint8"),
+    "rq": ("sbuf", [128, N * W], CODE), "rs": ("sbuf", [128, N * W], "uint8"),
+    "cq": ("sbuf", [128, N * W], CODE), "cs": ("sbuf", [128, N * W], "uint8"),
+    "uq": ("sbuf", [128, W], CODE), "us": ("sbuf", [128, W], "uint8"),
+    "vq": ("sbuf", [128, W], CODE), "vs": ("sbuf", [128, W], "uint8"),
+    "z": ("psum", [128, 2048], "float32"),
+    "yp": ("psum", [128, 2048], "float32"),
+}
+SEMAPHORES = ([a + str(k) for k in range(N) for a in ("a", "cq", "cs", "ym", "yc")]
+              + [a + str(k) for k in range(4) for a in ("z", "m", "r")] + [a + str(k) for k in range(3) for a in ("ld", "qd")]
+              + ["uq", "us", "loc", "loc2", "ldx", "ldw", "e0", "e1", "l0", "l1", "sqd", "xqd", "hqd", "sth", "sty"])
+RATE = float(np.float32(0.01425))
+
+
+def engines(m):
+    return [k for k in range(m.bit_length()) if m >> k & 1]
+
+
+def to_mask(es):
+    return sum(1 << e for e in es)
+
+
+def build(cores, topo):
+    everyone = range(128)
+    chips = []
+    for c in cores:
+        if topo.chip(c) not in chips:
+            chips.append(topo.chip(c))
+    on = {ch: [r for r in range(N) if topo.chip(cores[r]) == ch] for ch in chips}
+    calls, groups, relay, taken = {}, {}, {}, set(cores)
+    for r in range(N):
+        me = cores[r]
+        i = chips.index(topo.chip(me))
+        others = [chips[(i + k) % len(chips)] for k in range(1, len(chips))]
+        for ch in others:
+            for n, d in enumerate(on[ch]):
+                if topo.may_write(me, cores[d]):
+                    continue
+                where = topo.chip(me) if n == 0 else [
+                    k for k in sorted(set(topo.chip(c) for c in everyone)) if topo.mates(k, ch)][0]
+                h = [c for c in everyone if topo.chip(c) == where and c not in taken and topo.die(c) == topo.die(me)
+                     and topo.may_write(me, c) and topo.may_write(c, cores[d])][0]
+                taken.add(h)
+                relay[(r, d)] = h
+        others.sort(key=lambda ch: (r, on[ch][0]) not in relay)
+        partner = [d for d in on[topo.chip(me)] if d != r][0]
+        groups[r] = [list(on[ch]) for ch in others] + [[partner, r]]
+
+    def split_engines(me):
+        far = [c for c in everyone if topo.chip(c) != topo.chip(me)][0]
+        near = [c for c in everyone if topo.chip(c) == topo.chip(me) and c != me][0]
+        off = engines(topo.mask(me, far))
+        return off, [e for e in engines(topo.mask(me, near)) if e not in off]
+
+    def tr(src, cols, dst, eng, sem):
+        return {"src": src, "cols": cols, "dst": dst, "eng": eng, "sem": sem}
+
+    def call(lst, kind, loc, after, trs):
+        lst.append({"kind": kind, "loc": loc, "after": after, "tr": trs})
+
+    for r in range(N):
+        me = cores[r]
+        off, inner = split_engines(me)
+        rel = [k for k in (0, 1) if (r, groups[r][k][0]) in relay]
+        direct = [k for k in (0, 1) if k not in rel]
+        close = [relay[(r, d)] for k in rel for d in groups[r][k] if topo.chip(relay[(r, d)]) == topo.chip(me)]
+        away = [relay[(r, d)] for k in rel for d in groups[r][k] if relay[(r, d)] not in close]
+        half = len(inner) // 2
+        mine = inner if rel else inner[:half]
+        partner = groups[r][2][0]
+        lst = calls[me] = []
+
+        def hop(k, kind, part):
+            return [tr(("g", W * (2 * k + i)), W, [(relay[(r, d)], "u", 0)],
+                       (inner if relay[(r, d)] in close else off)[half * part:half * part + half], "u" + kind)
+                    for i, d in enumerate(groups[r][k])]
+        for k in rel:
+            call(lst, "s", "loc", ["qd%d" % k], hop(k, "s", 0))
+        if rel:
+            call(lst, "q", "loc", [], [t for k in rel for t in hop(k, "q", k)])
+
+        def straight(ks):
+            ends = [(k, i) for k in ks for i in (0, 1)]
+            n = len(off) // max(1, len(ends))
+            return [tr(("g", W * (2 * k + i)), W, [(cores[groups[r][k][i]], "r", W * r)], off[n * t:n * t + n],
+                       "a%d" % r) for t, (k, i) in enumerate(ends)]
+        home = tr(("g", 4 * W), W, [(cores[partner], "r", W * r)], mine, "a%d" % r)
+        for k in direct[:-1]:
+            call(lst, "q", "loc", ["qd%d" % k], straight([k]))
+        call(lst, "q", "loc", ["qd%d" % k for k in direct[-1:]] + ["qd2"], straight(direct[-1:]) + [home])
+        call(lst, "s", "loc", [], straight(direct) + [home])
+        out = [(h, "v", 0) for h in away] + [(cores[d], "c", W * r) for k in direct for d in groups[r][k]]
+        stay = [(h, "v", 0) for h in close] + [(cores[partner], "c", W * r)]
+        for kind in "qs":
+            call(lst, kind, "loc2", ["hqd"] if kind == "q" else [],
+                 [tr(("h", 0), W, d, e, "c%s%d" % (kind, r)) for d, e in ((out, off), (stay, mine))])
+    for (r, d), h in relay.items():
+        off, _ = split_engines(h)
+        lst = calls[h] = []
+        for kind in "sq":
+            call(lst, kind, "loc", ["u" + kind], [tr(("u", 0), W, [(cores[d], "r", W * r)], off, "a%d" % r)])
+        for kind in "qs":
+            sem = "c%s%d" % (kind, r)
+            call(lst, kind, "loc2", [sem], [tr(("v", 0), W, [(cores[d], "c", W * r)], off, sem)])
+    arrivals = {}
+    for r in range(N):
+        mychip = topo.chip(cores[r])
+        arrivals[r] = sorted([s for s in range(N) if s != r],
+                             key=lambda s: (topo.chip(cores[s]) != mychip, (s, r) in relay, s))
+    return calls, groups, arrivals
+
+
+def expected(calls):
+    got = {}
+    for core, lst in calls.items():
+        for c in lst:
+            for t in c["tr"]:
+                for key in [(d, t["sem"]) for d, _, _ in t["dst"]] + [(core, c["loc"])]:
+                    got[key] = got.get(key, 0) + len(t["eng"])
+    return got
+
+
+def remote(g, core, T, topo, calls, got):
+    def view(buf, kind, a, n):
+        v = T[buf + kind][:, a:a + n]
+        return v.bitcast(dt.uint8) if kind == "q" else v
+
+    def ident(c):
+        rid, pid, _ = topo.addr(c)
+        return DstId(rid=rid, pnc=pid)
+
+    for c in calls[core]:
+        for s in c["after"]:
+            g.wait_ge(T.sem[s], got.get((core, s), 1))
+        g.remote_dma_fused([RemoteDMATransfer(
+            dst_ids=[ident(d) for d, _, _ in t["dst"]], dma_engine_mask=to_mask(t["eng"]), remote_sem=T.sem[t["sem"]],
+            srcs=[view(t["src"][0], c["kind"], t["src"][1], t["cols"])],
+            dsts=[view(b, c["kind"], a, t["cols"]) for _, b, a in t["dst"]]) for t in c["tr"]],
+            local_sem=T.sem[c["loc"]])
+    for s in ("loc", "loc2"):
+        g.wait_ge(T.sem[s], got[(core, s)])
+
+
+def rank_program(g, core, T, topo):
+    calls, groups, arrivals = build(T.cores, topo)
+    if core not in calls:
+        return
+    got = expected(calls)
+    r = T.rank_of(core)
+    if r is None:
+        remote(g, core, T, topo, calls, got)
+        return
+    sem = T.sem
+
+    for k in range(3):
+        for q, i in ((g.sync, 0), (g.scalar, 1)):
+            c = groups[r][k][i]
+            s = 512 * (2 * k + i)
+            q.dma_start(T.bt[:, s:s + 512], T.b[:, 512 * c:512 * c + 512]).then_inc(sem["ld%d" % k], 16)
+    g.scalar.dma_start(T.wt[:], T.w[:]).then_inc(sem.ldw, 16)
+    g.sync.dma_start(T.xt[:], T.x[:]).then_inc(sem.ldx, 16)
+
+    v = g.vector
+    v.memset(T.eye[:], 1.0).then_inc(sem.e0, 1)
+    v.memset(T.pickt[:], 0.0).then_inc(sem.l0, 1)
+    g.wait_ge(sem.e0, 1)
+    g.affine_select(T.eye[:], T.eye[:], [[-1, 128]], AluOpType.is_equal, 0.0, 0, 1).then_inc(sem.e1, 1)
+    remote(g, core, T, topo, calls, got)
+
+    for k in range(3):
+        v.wait_ge(sem["ld%d" % k], 32)
+        v.quantize_mx(T.gq[:, 2 * W * k:2 * W * k + 2 * W], T.gs[:, 2 * W * k:2 * W * k + 2 * W],
+                      T.bt[:, 1024 * k:1024 * k + 1024]).then_inc(sem["qd%d" % k], 1)
+    v.wait_ge(sem.e1, 1)
+    v.wait_ge(sem.l0, 1)
+    v.tensor_copy(T.pickt[:, 3:515:4], T.eye[:]).then_inc(sem.l1, 1)
+    v.wait_ge(sem.l1, 1)
+    for b in range(4):
+        v.quantize_mx(T.sq[:, W * b:W * b + W], T.ss[:, W * b:W * b + W],
+                      T.pickt[:, 3 - b:515 - b]).then_inc(sem.sqd, 1)
+    v.wait_ge(sem.ldx, 16)
+    v.quantize_mx(T.xq[:], T.xs[:], T.xt[:]).then_inc(sem.xqd, 1)
+
+    pe = g.tensor
+    pe.wait_ge(sem.sqd, 4)
+    order = [r] + arrivals[r]
+    for n, s in enumerate(order):
+        if s == r:
+            pe.wait_ge(sem.qd2, 1)
+            q, p = T.gq[:, 5 * W:6 * W], T.gs[:, 5 * W:6 * W]
+        else:
+            pe.wait_ge(sem["a%d" % s], got[(core, "a%d" % s)])
+            q, p = T.rq[:, W * s:W * s + W], T.rs[:, W * s:W * s + W]
+        for b in range(4):
+            i = pe.matmul_mx(T.z[:, 512 * b:512 * b + W], T.sq[:, W * b:W * b + W], T.ss[:, W * b:W * b + W],
+                             q, p, n == 0, n == N - 1)
+            if n == N - 1:
+                i.then_inc(sem["z%d" % b], 1)
+
+    v.wait_ge(sem.ldw, 16)
+    for b in range(4):
+        g.scalar.wait_ge(sem["z%d" % b], 1)
+        g.scalar.activation(T.zc[:, W * b:W * b + W], T.z[:, 512 * b:512 * b + W], ActivationFunctionType.Identity,
+                            scale=RATE).then_inc(sem["m%d" % b], 1)
+        v.wait_ge(sem["m%d" % b], 1)
+        v.tensor_tensor(T.ht[:, b:512:4], T.wt[:, b:512:4], T.zc[:, W * b:W * b + W],
+                        AluOpType.subtract).then_inc(sem["r%d" % b], 1)
+    for b in range(4):
+        v.wait_ge(sem["r%d" % b], 1)
+    v.quantize_mx(T.hq[:], T.hs[:], T.ht[:]).then_inc(sem.hqd, 1)
+
+    for b in range(4):
+        g.scalar.wait_ge(sem["r%d" % b], 1)
+    g.scalar.wait_ge(sem.loc2, got[(core, "loc2")])
+    g.scalar.dma_start(T.h[:], T.ht[:]).then_inc(sem.sth, 16)
+
+    pe.wait_ge(sem.xqd, 1)
+    for n, s in enumerate(order):
+        if s == r:
+            pe.wait_ge(sem.hqd, 1)
+            q, p = T.hq[:], T.hs[:]
+        else:
+            for kind in "qs":
+                pe.wait_ge(sem["c%s%d" % (kind, s)], got[(core, "c%s%d" % (kind, s))])
+            q, p = T.cq[:, W * s:W * s + W], T.cs[:, W * s:W * s + W]
+        bank = T.yp[:, 512 * n:512 * n + W] if n < 4 else T.z[:, 512 * (n - 4):512 * (n - 4) + W]
+        pe.matmul_mx(bank, q, p, T.xq[:], T.xs[:], True, True).then_inc(sem["ym%d" % n], 1)
+        v.wait_ge(sem["ym%d" % n], 1)
+        v.tensor_copy(T.yt[:, W * s:W * s + W], bank).then_inc(sem["yc%d" % n], 1)
+        g.sync.wait_ge(sem["yc%d" % n], 1)
+        g.sync.dma_start(T.y[:, W * s:W * s + W], T.yt[:, W * s:W * s + W]).then_inc(sem.sty, 16)
+    g.scalar.wait_ge(sem.sth, 16)
+    g.sync.wait_ge(sem.sty, 16 * N)

@@ -4,6 +4,7 @@ from concourse.mybir import dt, AluOpType, ActivationFunctionType
 
 N = 6
 W = 128
+HELPED = 3
 CODE = "float8_e4m3fn_x4"
 SCRATCH = {
     "bt": ("sbuf", [128, N * 512], "bfloat16"),
@@ -27,7 +28,7 @@ SCRATCH = {
 }
 SEMAPHORES = ([a + str(k) for k in range(N) for a in ("a", "cq", "cs", "ym", "yc")]
               + [a + str(k) for k in range(4) for a in ("z", "m", "r")] + [a + str(k) for k in range(3) for a in ("ld", "qd")]
-              + ["uq", "us", "loc", "loc2", "ldx", "ldw", "e0", "e1", "l0", "l1", "sqd", "xqd", "hqd", "sth", "sty"])
+              + ["uq", "us", "loc", "loc2", "ldx", "ldw", "e0", "e1", "l0", "sp", "sx", "sqd", "xqd", "hqd", "sth", "sty"])
 RATE = float(np.float32(0.01425))
 
 
@@ -37,6 +38,17 @@ def engines(m):
 
 def to_mask(es):
     return sum(1 << e for e in es)
+
+
+def pieces(es, n):
+    size = len(es)
+    while size * n > len(es):
+        size //= 2
+    return [es[size * i:size * i + size] for i in range(n)]
+
+
+def made(r, partner):
+    return [0 if r < partner else 1, 2]
 
 
 def build(cores, topo):
@@ -77,46 +89,66 @@ def build(cores, topo):
     def call(lst, kind, loc, after, trs):
         lst.append({"kind": kind, "loc": loc, "after": after, "tr": trs})
 
-    for r in range(N):
+    def rank_calls(r):
         me = cores[r]
         off, inner = split_engines(me)
         rel = [k for k in (0, 1) if (r, groups[r][k][0]) in relay]
         direct = [k for k in (0, 1) if k not in rel]
         close = [relay[(r, d)] for k in rel for d in groups[r][k] if topo.chip(relay[(r, d)]) == topo.chip(me)]
         away = [relay[(r, d)] for k in rel for d in groups[r][k] if relay[(r, d)] not in close]
-        half = len(inner) // 2
-        mine = inner if rel else inner[:half]
+        mine = inner if rel else inner[:len(inner) // 2]
         partner = groups[r][2][0]
+        first = W * made(r, partner)[0]
         lst = calls[me] = []
 
-        def hop(k, kind, part):
-            return [tr(("g", W * (2 * k + i)), W, [(relay[(r, d)], "u", 0)],
-                       (inner if relay[(r, d)] in close else off)[half * part:half * part + half], "u" + kind)
-                    for i, d in enumerate(groups[r][k])]
-        for k in rel:
-            call(lst, "s", "loc", ["qd%d" % k], hop(k, "s", 0))
-        if rel:
-            call(lst, "q", "loc", [], [t for k in rel for t in hop(k, "q", k)])
+        def pick(eng):
+            return [tr(("s", first), W, [(cores[partner], "s", first)], eng, "sx")]
+
+        def tile(k, i, dst, buf, col, eng, sem):
+            return tr(("g", W * (2 * k + i)), W, [(dst, buf, col)], eng, sem)
+
+        def hop(ks, kind, spare):
+            ends = [(k, i, relay[(r, groups[r][k][i])]) for k in ks for i in (0, 1)]
+            ins = pieces(inner, sum(h in close for _, _, h in ends) + spare)
+            outs = pieces(off, sum(h in away for _, _, h in ends))
+            return [tile(k, i, h, "u", 0, (ins if h in close else outs).pop(0), "u" + kind) for k, i, h in ends], ins
 
         def straight(ks):
             ends = [(k, i) for k in ks for i in (0, 1)]
-            n = len(off) // max(1, len(ends))
-            return [tr(("g", W * (2 * k + i)), W, [(cores[groups[r][k][i]], "r", W * r)], off[n * t:n * t + n],
-                       "a%d" % r) for t, (k, i) in enumerate(ends)]
-        home = tr(("g", 4 * W), W, [(cores[partner], "r", W * r)], mine, "a%d" % r)
+            es = pieces(off, max(1, len(ends)))
+            return [tile(k, i, cores[groups[r][k][i]], "r", W * r, es.pop(0), "a%d" % r) for k, i in ends]
+
+        def home(eng):
+            return [tile(2, 0, cores[partner], "r", W * r, eng, "a%d" % r)]
+
+        call(lst, "q", "loc", ["sp"], pick(off + inner if rel else off))
+        for k in rel:
+            call(lst, "q", "loc", ["qd%d" % k], hop([k], "q", 0)[0])
+        if rel:
+            t, rest = hop(rel, "s", 1)
+            call(lst, "s", "loc", [], t + pick(rest[0]))
         for k in direct[:-1]:
             call(lst, "q", "loc", ["qd%d" % k], straight([k]))
-        call(lst, "q", "loc", ["qd%d" % k for k in direct[-1:]] + ["qd2"], straight(direct[-1:]) + [home])
-        call(lst, "s", "loc", [], straight(direct) + [home])
+        call(lst, "q", "loc", ["qd%d" % k for k in direct[-1:]] + ["qd2"], straight(direct[-1:]) + home(mine))
+        two = pieces(mine, 1 if rel else 2)
+        call(lst, "s", "loc", [], straight(direct) + home(two[0]) + ([] if rel else pick(two[1])))
         out = [(h, "v", 0) for h in away] + [(cores[d], "c", W * r) for k in direct for d in groups[r][k]]
         stay = [(h, "v", 0) for h in close] + [(cores[partner], "c", W * r)]
         for kind in "qs":
             call(lst, kind, "loc2", ["hqd"] if kind == "q" else [],
                  [tr(("h", 0), W, d, e, "c%s%d" % (kind, r)) for d, e in ((out, off), (stay, mine))])
+
+    for r in range(N):
+        rank_calls(r)
     for (r, d), h in relay.items():
         off, _ = split_engines(h)
         lst = calls[h] = []
-        for kind in "sq":
+        peers = [x for e, x in relay.items() if e[1] == d]
+        cols = W // len(peers)
+        at = W * HELPED + cols * peers.index(h)
+        for kind in "qs":
+            call(lst, kind, "loc", ["sp"] if kind == "q" else [], [tr(("s", at), cols, [(cores[d], "s", at)], off, "sx")])
+        for kind in "qs":
             call(lst, kind, "loc", ["u" + kind], [tr(("u", 0), W, [(cores[d], "r", W * r)], off, "a%d" % r)])
         for kind in "qs":
             sem = "c%s%d" % (kind, r)
@@ -166,10 +198,26 @@ def rank_program(g, core, T, topo):
         return
     got = expected(calls)
     r = T.rank_of(core)
+    sem = T.sem
+    v = g.vector
+
+    def diagonal():
+        v.memset(T.pickt[:], 0.0).then_inc(sem.l0, 1)
+        v.memset(T.eye[:], 1.0).then_inc(sem.e0, 1)
+        g.wait_ge(sem.l0, 1)
+        g.wait_ge(sem.e0, 1)
+        g.affine_select(T.pickt[:, 3:515:4], T.eye[:], [[-1, 128]], AluOpType.is_equal, 0.0, 0, 1).then_inc(sem.e1, 1)
+        v.wait_ge(sem.e1, 1)
+
+    def pick(b, done):
+        v.quantize_mx(T.sq[:, W * b:W * b + W], T.ss[:, W * b:W * b + W], T.pickt[:, 3 - b:515 - b]).then_inc(done, 1)
+
     if r is None:
+        diagonal()
+        pick(HELPED, sem.sp)
         remote(g, core, T, topo, calls, got)
         return
-    sem = T.sem
+    own = made(r, groups[r][2][0])
 
     for k in range(3):
         for q, i in ((g.sync, 0), (g.scalar, 1)):
@@ -177,31 +225,23 @@ def rank_program(g, core, T, topo):
             s = 512 * (2 * k + i)
             q.dma_start(T.bt[:, s:s + 512], T.b[:, 512 * c:512 * c + 512]).then_inc(sem["ld%d" % k], 16)
     g.scalar.dma_start(T.wt[:], T.w[:]).then_inc(sem.ldw, 16)
+    g.sync.wait_ge(sem.loc, got[(core, "loc")])
     g.sync.dma_start(T.xt[:], T.x[:]).then_inc(sem.ldx, 16)
 
-    v = g.vector
-    v.memset(T.eye[:], 1.0).then_inc(sem.e0, 1)
-    v.memset(T.pickt[:], 0.0).then_inc(sem.l0, 1)
-    g.wait_ge(sem.e0, 1)
-    g.affine_select(T.eye[:], T.eye[:], [[-1, 128]], AluOpType.is_equal, 0.0, 0, 1).then_inc(sem.e1, 1)
+    diagonal()
+    pick(own[0], sem.sp)
     remote(g, core, T, topo, calls, got)
 
     for k in range(3):
         v.wait_ge(sem["ld%d" % k], 32)
         v.quantize_mx(T.gq[:, 2 * W * k:2 * W * k + 2 * W], T.gs[:, 2 * W * k:2 * W * k + 2 * W],
                       T.bt[:, 1024 * k:1024 * k + 1024]).then_inc(sem["qd%d" % k], 1)
-    v.wait_ge(sem.e1, 1)
-    v.wait_ge(sem.l0, 1)
-    v.tensor_copy(T.pickt[:, 3:515:4], T.eye[:]).then_inc(sem.l1, 1)
-    v.wait_ge(sem.l1, 1)
-    for b in range(4):
-        v.quantize_mx(T.sq[:, W * b:W * b + W], T.ss[:, W * b:W * b + W],
-                      T.pickt[:, 3 - b:515 - b]).then_inc(sem.sqd, 1)
-    v.wait_ge(sem.ldx, 16)
-    v.quantize_mx(T.xq[:], T.xs[:], T.xt[:]).then_inc(sem.xqd, 1)
+    pick(own[1], sem.sqd)
 
     pe = g.tensor
-    pe.wait_ge(sem.sqd, 4)
+    pe.wait_ge(sem.sp, 1)
+    pe.wait_ge(sem.sqd, 1)
+    picks = own + [b for b in range(4) if b not in own]
     order = [r] + arrivals[r]
     for n, s in enumerate(order):
         if s == r:
@@ -210,14 +250,16 @@ def rank_program(g, core, T, topo):
         else:
             pe.wait_ge(sem["a%d" % s], got[(core, "a%d" % s)])
             q, p = T.rq[:, W * s:W * s + W], T.rs[:, W * s:W * s + W]
-        for b in range(4):
+        for b in picks:
+            if n == 0 and b == picks[len(own)]:
+                pe.wait_ge(sem.sx, got[(core, "sx")])
             i = pe.matmul_mx(T.z[:, 512 * b:512 * b + W], T.sq[:, W * b:W * b + W], T.ss[:, W * b:W * b + W],
                              q, p, n == 0, n == N - 1)
             if n == N - 1:
                 i.then_inc(sem["z%d" % b], 1)
 
     v.wait_ge(sem.ldw, 16)
-    for b in range(4):
+    for b in picks:
         g.scalar.wait_ge(sem["z%d" % b], 1)
         g.scalar.activation(T.zc[:, W * b:W * b + W], T.z[:, 512 * b:512 * b + W], ActivationFunctionType.Identity,
                             scale=RATE).then_inc(sem["m%d" % b], 1)
@@ -227,6 +269,8 @@ def rank_program(g, core, T, topo):
     for b in range(4):
         v.wait_ge(sem["r%d" % b], 1)
     v.quantize_mx(T.hq[:], T.hs[:], T.ht[:]).then_inc(sem.hqd, 1)
+    v.wait_ge(sem.ldx, 16)
+    v.quantize_mx(T.xq[:], T.xs[:], T.xt[:]).then_inc(sem.xqd, 1)
 
     for b in range(4):
         g.scalar.wait_ge(sem["r%d" % b], 1)
@@ -234,7 +278,7 @@ def rank_program(g, core, T, topo):
     g.scalar.dma_start(T.h[:], T.ht[:]).then_inc(sem.sth, 16)
 
     pe.wait_ge(sem.xqd, 1)
-    for n, s in enumerate(order):
+    for n, s in enumerate(arrivals[r][:1] + [r] + arrivals[r][1:]):
         if s == r:
             pe.wait_ge(sem.hqd, 1)
             q, p = T.hq[:], T.hs[:]

@@ -5,6 +5,15 @@ from concourse.mybir import dt, AluOpType, ActivationFunctionType
 N = 6
 W = 128
 HELPED = 3
+ROADS = {(0, 1): ("own", "same"), (0, 5): ("mate", "other"),
+         (1, 2): ("own", "same"), (1, 0): ("mate", "same"),
+         (2, 0): ("own", "same"), (2, 3): ("own", "same"), (2, 4): ("mate", "same"),
+         (3, 1): ("own", "same"), (3, 4): ("mate", "same"),
+         (4, 0): ("own", "same"), (4, 5): ("own", "same"), (4, 2): ("mate", "other"), (4, 3): ("mate", "same"),
+         (5, 1): ("own", "same"), (5, 4): ("mate", "same")}
+Z_ORDER = [[3, 5, 2, 4, 1], [4, 2, 0, 3, 5], [5, 0, 4, 3, 1], [0, 1, 5, 4, 2], [1, 0, 3, 5, 2], [2, 1, 3, 4, 0]]
+Z_ORDER[4][:2], Z_ORDER[5][:2] = [0, 1], [1, 2]
+Y_ORDER = [[3, 5, 1, 2, 4], [2, 4, 5, 3, 0], [5, 3, 4, 0, 1], [0, 1, 5, 4, 2], [1, 2, 0, 5, 3], [2, 1, 3, 0, 4]]
 CODE = "float8_e4m3fn_x4"
 SCRATCH = {
     "bt": ("sbuf", [128, N * 512], "bfloat16"),
@@ -59,23 +68,28 @@ def build(cores, topo):
             chips.append(topo.chip(c))
     on = {ch: [r for r in range(N) if topo.chip(cores[r]) == ch] for ch in chips}
     calls, groups, relay, taken = {}, {}, {}, set(cores)
+
+    def rest(r):
+        i = chips.index(topo.chip(cores[r]))
+        return [chips[(i + k) % len(chips)] for k in range(1, len(chips))]
+
+    def reach(c):
+        return sum(topo.may_write(c, d) for d in everyone)
+
+    for r, d in sorted(ROADS, key=lambda e: (topo.may_write(cores[e[0]], cores[e[1]]), e)):
+        place, side = ROADS[(r, d)]
+        mine, its = topo.chip(cores[r]), topo.chip(cores[d])
+        where = [ch for ch in sorted(set(topo.chip(c) for c in everyone))
+                 if (ch == mine if place == "own" else topo.mates(ch, its))][0]
+        free = [c for c in everyone if topo.chip(c) == where and c not in taken
+                and (topo.die(c) == topo.die(cores[r])) == (side == "same")
+                and topo.may_write(cores[r], c) and topo.may_write(c, cores[d])]
+        relay[(r, d)] = min(free, key=reach)
+        taken.add(relay[(r, d)])
     for r in range(N):
-        me = cores[r]
-        i = chips.index(topo.chip(me))
-        others = [chips[(i + k) % len(chips)] for k in range(1, len(chips))]
-        for ch in others:
-            for n, d in enumerate(on[ch]):
-                if topo.may_write(me, cores[d]):
-                    continue
-                where = topo.chip(me) if n == 0 else [
-                    k for k in sorted(set(topo.chip(c) for c in everyone)) if topo.mates(k, ch)][0]
-                h = [c for c in everyone if topo.chip(c) == where and c not in taken and topo.die(c) == topo.die(me)
-                     and topo.may_write(me, c) and topo.may_write(c, cores[d])][0]
-                taken.add(h)
-                relay[(r, d)] = h
-        others.sort(key=lambda ch: (r, on[ch][0]) not in relay)
-        partner = [d for d in on[topo.chip(me)] if d != r][0]
-        groups[r] = [list(on[ch]) for ch in others] + [[partner, r]]
+        others = sorted(rest(r), key=lambda ch: all((r, d) not in relay for d in on[ch]))
+        partner = [d for d in on[topo.chip(cores[r])] if d != r][0]
+        groups[r] = [sorted(on[ch], key=lambda d: (r, d) not in relay) for ch in others] + [[partner, r]]
 
     def split_engines(me):
         far = [c for c in everyone if topo.chip(c) != topo.chip(me)][0]
@@ -92,51 +106,43 @@ def build(cores, topo):
     def rank_calls(r):
         me = cores[r]
         off, inner = split_engines(me)
-        rel = [k for k in (0, 1) if (r, groups[r][k][0]) in relay]
-        direct = [k for k in (0, 1) if k not in rel]
-        close = [relay[(r, d)] for k in rel for d in groups[r][k] if topo.chip(relay[(r, d)]) == topo.chip(me)]
-        away = [relay[(r, d)] for k in rel for d in groups[r][k] if relay[(r, d)] not in close]
-        mine = inner if rel else inner[:len(inner) // 2]
         partner = groups[r][2][0]
         first = W * made(r, partner)[0]
         lst = calls[me] = []
 
-        def pick(eng):
-            return [tr(("s", first), W, [(cores[partner], "s", first)], eng, "sx")]
+        def close(c):
+            return topo.chip(c) == topo.chip(me)
 
-        def tile(k, i, dst, buf, col, eng, sem):
-            return tr(("g", W * (2 * k + i)), W, [(dst, buf, col)], eng, sem)
+        def deal(ends, kind):
+            went = []
+            for k, i in ends:
+                d = groups[r][k][i]
+                h = relay.get((r, d))
+                to = (cores[d], "r", W * r, "a%d" % r) if h is None else (h, "u", 0, "u" + kind)
+                went.append((("g", W * (2 * k + i)),) + to)
+            ins = pieces(inner, max(1, sum(close(x[1]) for x in went)))
+            outs = pieces(off, max(1, sum(not close(x[1]) for x in went)))
+            return [tr(src, W, [(c, buf, col)], (ins if close(c) else outs).pop(0), s) for src, c, buf, col, s in went]
 
-        def hop(ks, kind, spare):
-            ends = [(k, i, relay[(r, groups[r][k][i])]) for k in ks for i in (0, 1)]
-            ins = pieces(inner, sum(h in close for _, _, h in ends) + spare)
-            outs = pieces(off, sum(h in away for _, _, h in ends))
-            return [tile(k, i, h, "u", 0, (ins if h in close else outs).pop(0), "u" + kind) for k, i, h in ends], ins
-
-        def straight(ks):
-            ends = [(k, i) for k in ks for i in (0, 1)]
-            es = pieces(off, max(1, len(ends)))
-            return [tile(k, i, cores[groups[r][k][i]], "r", W * r, es.pop(0), "a%d" % r) for k, i in ends]
-
-        def home(eng):
-            return [tile(2, 0, cores[partner], "r", W * r, eng, "a%d" % r)]
-
-        call(lst, "q", "loc", ["sp"], pick(off + inner if rel else off))
-        for k in rel:
-            call(lst, "q", "loc", ["qd%d" % k], hop([k], "q", 0)[0])
-        if rel:
-            t, rest = hop(rel, "s", 1)
-            call(lst, "s", "loc", [], t + pick(rest[0]))
-        for k in direct[:-1]:
-            call(lst, "q", "loc", ["qd%d" % k], straight([k]))
-        call(lst, "q", "loc", ["qd%d" % k for k in direct[-1:]] + ["qd2"], straight(direct[-1:]) + home(mine))
-        two = pieces(mine, 1 if rel else 2)
-        call(lst, "s", "loc", [], straight(direct) + home(two[0]) + ([] if rel else pick(two[1])))
-        out = [(h, "v", 0) for h in away] + [(cores[d], "c", W * r) for k in direct for d in groups[r][k]]
-        stay = [(h, "v", 0) for h in close] + [(cores[partner], "c", W * r)]
-        for kind in "qs":
-            call(lst, kind, "loc2", ["hqd"] if kind == "q" else [],
-                 [tr(("h", 0), W, d, e, "c%s%d" % (kind, r)) for d, e in ((out, off), (stay, mine))])
+        picked = [tr(("s", first), W, [(cores[partner], "s", first)], off + inner, "sx")]
+        call(lst, "q", "loc", ["sp"], picked)
+        for k, ends in enumerate(([(0, 0), (0, 1)], [(1, 0), (1, 1)], [(2, 0)])):
+            for kind in "qs":
+                call(lst, kind, "loc", ["qd%d" % k] if kind == "q" else [], deal(ends, kind))
+            if k == 0:
+                call(lst, "s", "loc", [], picked)
+        first_of, then_of = [], []
+        for eng, near in ((off, False), (inner, True)):
+            hs = [(h, "v", 0) for (s, _), h in relay.items() if s == r and close(h) == near]
+            rs = [(cores[d], "c", W * r) for d in groups[r][0] + groups[r][1] + [partner]
+                  if (r, d) not in relay and close(cores[d]) == near]
+            for part, dst in ((first_of, hs or rs), (then_of, rs if hs else [])):
+                if dst:
+                    part.append((dst, eng))
+        for part in (first_of, then_of):
+            for kind in "qs":
+                call(lst, kind, "loc2", ["hqd"] if kind == "q" else [],
+                     [tr(("h", 0), W, d, e, "c%s%d" % (kind, r)) for d, e in part])
 
     for r in range(N):
         rank_calls(r)
@@ -144,8 +150,9 @@ def build(cores, topo):
         off, _ = split_engines(h)
         lst = calls[h] = []
         peers = [x for e, x in relay.items() if e[1] == d]
-        cols = W // len(peers)
-        at = W * HELPED + cols * peers.index(h)
+        ends = [16 * (W // 16 * k // len(peers)) for k in range(len(peers) + 1)]
+        k = peers.index(h)
+        at, cols = W * HELPED + ends[k], ends[k + 1] - ends[k]
         for kind in "qs":
             call(lst, kind, "loc", ["sp"] if kind == "q" else [], [tr(("s", at), cols, [(cores[d], "s", at)], off, "sx")])
         for kind in "qs":
@@ -153,12 +160,7 @@ def build(cores, topo):
         for kind in "qs":
             sem = "c%s%d" % (kind, r)
             call(lst, kind, "loc2", [sem], [tr(("v", 0), W, [(cores[d], "c", W * r)], off, sem)])
-    arrivals = {}
-    for r in range(N):
-        mychip = topo.chip(cores[r])
-        arrivals[r] = sorted([s for s in range(N) if s != r],
-                             key=lambda s: (topo.chip(cores[s]) != mychip, (s, r) in relay, s))
-    return calls, groups, arrivals
+    return calls, groups
 
 
 def expected(calls):
@@ -193,7 +195,7 @@ def remote(g, core, T, topo, calls, got):
 
 
 def rank_program(g, core, T, topo):
-    calls, groups, arrivals = build(T.cores, topo)
+    calls, groups = build(T.cores, topo)
     if core not in calls:
         return
     got = expected(calls)
@@ -202,11 +204,12 @@ def rank_program(g, core, T, topo):
     v = g.vector
 
     def diagonal():
-        v.memset(T.pickt[:], 0.0).then_inc(sem.l0, 1)
         v.memset(T.eye[:], 1.0).then_inc(sem.e0, 1)
-        g.wait_ge(sem.l0, 1)
+        for k in range(3):
+            v.memset(T.pickt[:, k:516:4], 0.0).then_inc(sem.l0, 1)
         g.wait_ge(sem.e0, 1)
         g.affine_select(T.pickt[:, 3:515:4], T.eye[:], [[-1, 128]], AluOpType.is_equal, 0.0, 0, 1).then_inc(sem.e1, 1)
+        v.wait_ge(sem.l0, 3)
         v.wait_ge(sem.e1, 1)
 
     def pick(b, done):
@@ -242,21 +245,25 @@ def rank_program(g, core, T, topo):
     pe.wait_ge(sem.sp, 1)
     pe.wait_ge(sem.sqd, 1)
     picks = own + [b for b in range(4) if b not in own]
-    order = [r] + arrivals[r]
-    for n, s in enumerate(order):
+    order = [r] + Z_ORDER[r]
+
+    def part(s):
         if s == r:
             pe.wait_ge(sem.qd2, 1)
-            q, p = T.gq[:, 5 * W:6 * W], T.gs[:, 5 * W:6 * W]
-        else:
-            pe.wait_ge(sem["a%d" % s], got[(core, "a%d" % s)])
-            q, p = T.rq[:, W * s:W * s + W], T.rs[:, W * s:W * s + W]
+            return T.gq[:, 5 * W:6 * W], T.gs[:, 5 * W:6 * W]
+        pe.wait_ge(sem["a%d" % s], got[(core, "a%d" % s)])
+        return T.rq[:, W * s:W * s + W], T.rs[:, W * s:W * s + W]
+
+    for group in [[s] for s in order[:N - 2]] + [order[N - 2:]]:
+        held = [(s, part(s)) for s in group]
         for b in picks:
-            if n == 0 and b == picks[len(own)]:
+            if group[0] == r and b == picks[len(own)]:
                 pe.wait_ge(sem.sx, got[(core, "sx")])
-            i = pe.matmul_mx(T.z[:, 512 * b:512 * b + W], T.sq[:, W * b:W * b + W], T.ss[:, W * b:W * b + W],
-                             q, p, n == 0, n == N - 1)
-            if n == N - 1:
-                i.then_inc(sem["z%d" % b], 1)
+            for s, (q, p) in held:
+                i = pe.matmul_mx(T.z[:, 512 * b:512 * b + W], T.sq[:, W * b:W * b + W], T.ss[:, W * b:W * b + W],
+                                 q, p, s == r, s == order[-1])
+                if s == order[-1]:
+                    i.then_inc(sem["z%d" % b], 1)
 
     v.wait_ge(sem.ldw, 16)
     for b in picks:
@@ -278,7 +285,7 @@ def rank_program(g, core, T, topo):
     g.scalar.dma_start(T.h[:], T.ht[:]).then_inc(sem.sth, 16)
 
     pe.wait_ge(sem.xqd, 1)
-    for n, s in enumerate(arrivals[r][:1] + [r] + arrivals[r][1:]):
+    for n, s in enumerate(Y_ORDER[r][:1] + [r] + Y_ORDER[r][1:]):
         if s == r:
             pe.wait_ge(sem.hqd, 1)
             q, p = T.hq[:], T.hs[:]

import numpy as np
from concourse.bass import DstId, RemoteDMATransfer
from concourse.mybir import dt, AluOpType, ActivationFunctionType

N = 6
W = 128
HELPED = 3
ROADS = {(0, 1): ("own", "same"), (0, 5): ("mate", "other"),
         (1, 2): ("own", "same"), (1, 0): ("mate", "same"),
         (2, 0): ("own", "same"), (2, 3): ("own", "same"), (2, 4): ("mate", "same"),
         (3, 1): ("own", "same"), (3, 4): ("mate", "same"),
         (4, 0): ("own", "same"), (4, 5): ("own", "same"), (4, 2): ("mate", "other"), (4, 3): ("mate", "same"),
         (5, 1): ("own", "same"), (5, 4): ("mate", "same")}
Z_ORDER = [[3, 5, 2, 4, 1], [4, 2, 0, 3, 5], [5, 0, 4, 3, 1], [0, 1, 5, 4, 2], [1, 0, 3, 5, 2], [2, 1, 3, 4, 0]]
Z_ORDER[4][:2], Z_ORDER[5][:2] = [0, 1], [1, 2]
Y_ORDER = [[3, 5, 1, 2, 4], [2, 4, 5, 3, 0], [5, 3, 4, 0, 1], [0, 1, 5, 4, 2], [1, 2, 0, 5, 3], [2, 1, 3, 0, 4]]
CODE = "float8_e4m3fn_x4"
SCRATCH = {
    "bt": ("sbuf", [128, N * 512], "bfloat16"),
    "xt": ("sbuf", [128, 512], "bfloat16"),
    "wt": ("sbuf", [128, 512], "bfloat16"),
    "ht": ("sbuf", [128, 512], "bfloat16"),
    "eye": ("sbuf", [128, 128], "bfloat16"),
    "pickt": ("sbuf", [128, 516], "bfloat16"),
    "zc": ("sbuf", [128, 512], "float32"),
    "yt": ("sbuf", [128, N * W], "float32"),
    "gq": ("sbuf", [128, N * W], CODE), "gs": ("sbuf", [128, N * W], "uint8"),
    "sq": ("sbuf", [128, 4 * W], CODE), "ss": ("sbuf", [128, 4 * W], "uint8"),
    "xq": ("sbuf", [128, W], CODE), "xs": ("sbuf", [128, W], "uint8"),
    "hq": ("sbuf", [128, W], CODE), "hs": ("sbuf", [128, W], "uint8"),
    "rq": ("sbuf", [128, N * W], CODE), "rs": ("sbuf", [128, N * W], "uint8"),
    "cq": ("sbuf", [128, N * W], CODE), "cs": ("sbuf", [128, N * W], "uint8"),
    "uq": ("sbuf", [128, W], CODE), "us": ("sbuf", [128, W], "uint8"),
    "vq": ("sbuf", [128, W], CODE), "vs": ("sbuf", [128, W], "uint8"),
    "z": ("psum", [128, 2048], "float32"),
    "yp": ("psum", [128, 2048], "float32"),
}
SEMAPHORES = ([a + str(k) for k in range(N) for a in ("a", "cq", "cs", "ym", "yc")]
              + [a + str(k) for k in range(4) for a in ("z", "m", "r")] + [a + str(k) for k in range(3) for a in ("ld", "qd")]
              + ["uq", "us", "loc", "loc2", "ldx", "ldw", "e0", "e1", "l0", "sp", "sx", "sqd", "xqd", "hqd", "sth", "sty"])
RATE = float(np.float32(0.01425))


def engines(m):
    return [k for k in range(m.bit_length()) if m >> k & 1]


def to_mask(es):
    return sum(1 << e for e in es)


def pieces(es, n):
    size = len(es)
    while size * n > len(es):
        size //= 2
    return [es[size * i:size * i + size] for i in range(n)]


def made(r, partner):
    return [0 if r < partner else 1, 2]


def build(cores, topo):
    everyone = range(128)
    chips = []
    for c in cores:
        if topo.chip(c) not in chips:
            chips.append(topo.chip(c))
    on = {ch: [r for r in range(N) if topo.chip(cores[r]) == ch] for ch in chips}
    calls, groups, relay, taken = {}, {}, {}, set(cores)

    def rest(r):
        i = chips.index(topo.chip(cores[r]))
        return [chips[(i + k) % len(chips)] for k in range(1, len(chips))]

    def reach(c):
        return sum(topo.may_write(c, d) for d in everyone)

    for r, d in sorted(ROADS, key=lambda e: (topo.may_write(cores[e[0]], cores[e[1]]), e)):
        place, side = ROADS[(r, d)]
        mine, its = topo.chip(cores[r]), topo.chip(cores[d])
        where = [ch for ch in sorted(set(topo.chip(c) for c in everyone))
                 if (ch == mine if place == "own" else topo.mates(ch, its))][0]
        free = [c for c in everyone if topo.chip(c) == where and c not in taken
                and (topo.die(c) == topo.die(cores[r])) == (side == "same")
                and topo.may_write(cores[r], c) and topo.may_write(c, cores[d])]
        relay[(r, d)] = min(free, key=reach)
        taken.add(relay[(r, d)])
    for r in range(N):
        others = sorted(rest(r), key=lambda ch: all((r, d) not in relay for d in on[ch]))
        partner = [d for d in on[topo.chip(cores[r])] if d != r][0]
        groups[r] = [sorted(on[ch], key=lambda d: (r, d) not in relay) for ch in others] + [[partner, r]]

    def split_engines(me):
        far = [c for c in everyone if topo.chip(c) != topo.chip(me)][0]
        near = [c for c in everyone if topo.chip(c) == topo.chip(me) and c != me][0]
        off = engines(topo.mask(me, far))
        return off, [e for e in engines(topo.mask(me, near)) if e not in off]

    def tr(src, cols, dst, eng, sem):
        return {"src": src, "cols": cols, "dst": dst, "eng": eng, "sem": sem}

    def call(lst, kind, loc, after, trs):
        lst.append({"kind": kind, "loc": loc, "after": after, "tr": trs})

    def rank_calls(r):
        me = cores[r]
        off, inner = split_engines(me)
        partner = groups[r][2][0]
        first = W * made(r, partner)[0]
        lst = calls[me] = []

        def close(c):
            return topo.chip(c) == topo.chip(me)

        def deal(ends, kind):
            went = []
            for k, i in ends:
                d = groups[r][k][i]
                h = relay.get((r, d))
                to = (cores[d], "r", W * r, "a%d" % r) if h is None else (h, "u", 0, "u" + kind)
                went.append((("g", W * (2 * k + i)),) + to)
            ins = pieces(inner, max(1, sum(close(x[1]) for x in went)))
            outs = pieces(off, max(1, sum(not close(x[1]) for x in went)))
            return [tr(src, W, [(c, buf, col)], (ins if close(c) else outs).pop(0), s) for src, c, buf, col, s in went]

        picked = [tr(("s", first), W, [(cores[partner], "s", first)], off + inner, "sx")]
        call(lst, "q", "loc", ["sp"], picked)
        for k, ends in enumerate(([(0, 0), (0, 1)], [(1, 0), (1, 1)], [(2, 0)])):
            for kind in "qs":
                call(lst, kind, "loc", ["qd%d" % k] if kind == "q" else [], deal(ends, kind))
            if k == 0:
                call(lst, "s", "loc", [], picked)
        first_of, then_of = [], []
        for eng, near in ((off, False), (inner, True)):
            hs = [(h, "v", 0) for (s, _), h in relay.items() if s == r and close(h) == near]
            rs = [(cores[d], "c", W * r) for d in groups[r][0] + groups[r][1] + [partner]
                  if (r, d) not in relay and close(cores[d]) == near]
            for part, dst in ((first_of, hs or rs), (then_of, rs if hs else [])):
                if dst:
                    part.append((dst, eng))
        for part in (first_of, then_of):
            for kind in "qs":
                call(lst, kind, "loc2", ["hqd"] if kind == "q" else [],
                     [tr(("h", 0), W, d, e, "c%s%d" % (kind, r)) for d, e in part])

    for r in range(N):
        rank_calls(r)
    for (r, d), h in relay.items():
        off, _ = split_engines(h)
        lst = calls[h] = []
        peers = [x for e, x in relay.items() if e[1] == d]
        ends = [16 * (W // 16 * k // len(peers)) for k in range(len(peers) + 1)]
        k = peers.index(h)
        at, cols = W * HELPED + ends[k], ends[k + 1] - ends[k]
        for kind in "qs":
            call(lst, kind, "loc", ["sp"] if kind == "q" else [], [tr(("s", at), cols, [(cores[d], "s", at)], off, "sx")])
        for kind in "qs":
            call(lst, kind, "loc", ["u" + kind], [tr(("u", 0), W, [(cores[d], "r", W * r)], off, "a%d" % r)])
        for kind in "qs":
            sem = "c%s%d" % (kind, r)
            call(lst, kind, "loc2", [sem], [tr(("v", 0), W, [(cores[d], "c", W * r)], off, sem)])
    return calls, groups


def expected(calls):
    got = {}
    for core, lst in calls.items():
        for c in lst:
            for t in c["tr"]:
                for key in [(d, t["sem"]) for d, _, _ in t["dst"]] + [(core, c["loc"])]:
                    got[key] = got.get(key, 0) + len(t["eng"])
    return got


def remote(g, core, T, topo, calls, got):
    def view(buf, kind, a, n):
        v = T[buf + kind][:, a:a + n]
        return v.bitcast(dt.uint8) if kind == "q" else v

    def ident(c):
        rid, pid, _ = topo.addr(c)
        return DstId(rid=rid, pnc=pid)

    for c in calls[core]:
        for s in c["after"]:
            g.wait_ge(T.sem[s], got.get((core, s), 1))
        g.remote_dma_fused([RemoteDMATransfer(
            dst_ids=[ident(d) for d, _, _ in t["dst"]], dma_engine_mask=to_mask(t["eng"]), remote_sem=T.sem[t["sem"]],
            srcs=[view(t["src"][0], c["kind"], t["src"][1], t["cols"])],
            dsts=[view(b, c["kind"], a, t["cols"]) for _, b, a in t["dst"]]) for t in c["tr"]],
            local_sem=T.sem[c["loc"]])
    for s in ("loc", "loc2"):
        g.wait_ge(T.sem[s], got[(core, s)])


def rank_program(g, core, T, topo):
    calls, groups = build(T.cores, topo)
    if core not in calls:
        return
    got = expected(calls)
    r = T.rank_of(core)
    sem = T.sem
    v = g.vector

    def diagonal():
        v.memset(T.eye[:], 1.0).then_inc(sem.e0, 1)
        for k in range(3):
            v.memset(T.pickt[:, k:516:4], 0.0).then_inc(sem.l0, 1)
        g.wait_ge(sem.e0, 1)
        g.affine_select(T.pickt[:, 3:515:4], T.eye[:], [[-1, 128]], AluOpType.is_equal, 0.0, 0, 1).then_inc(sem.e1, 1)
        v.wait_ge(sem.l0, 3)
        v.wait_ge(sem.e1, 1)

    def pick(b, done):
        v.quantize_mx(T.sq[:, W * b:W * b + W], T.ss[:, W * b:W * b + W], T.pickt[:, 3 - b:515 - b]).then_inc(done, 1)

    if r is None:
        diagonal()
        pick(HELPED, sem.sp)
        remote(g, core, T, topo, calls, got)
        return
    own = made(r, groups[r][2][0])

    for k in range(3):
        for q, i in ((g.sync, 0), (g.scalar, 1)):
            c = groups[r][k][i]
            s = 512 * (2 * k + i)
            q.dma_start(T.bt[:, s:s + 512], T.b[:, 512 * c:512 * c + 512]).then_inc(sem["ld%d" % k], 16)
    g.scalar.dma_start(T.wt[:], T.w[:]).then_inc(sem.ldw, 16)
    g.sync.wait_ge(sem.loc, got[(core, "loc")])
    g.sync.dma_start(T.xt[:], T.x[:]).then_inc(sem.ldx, 16)

    diagonal()
    pick(own[0], sem.sp)
    remote(g, core, T, topo, calls, got)

    for k in range(3):
        v.wait_ge(sem["ld%d" % k], 32)
        v.quantize_mx(T.gq[:, 2 * W * k:2 * W * k + 2 * W], T.gs[:, 2 * W * k:2 * W * k + 2 * W],
                      T.bt[:, 1024 * k:1024 * k + 1024]).then_inc(sem["qd%d" % k], 1)
    pick(own[1], sem.sqd)

    pe = g.tensor
    pe.wait_ge(sem.sp, 1)
    pe.wait_ge(sem.sqd, 1)
    picks = own + [b for b in range(4) if b not in own]
    order = [r] + Z_ORDER[r]

    def part(s):
        if s == r:
            pe.wait_ge(sem.qd2, 1)
            return T.gq[:, 5 * W:6 * W], T.gs[:, 5 * W:6 * W]
        pe.wait_ge(sem["a%d" % s], got[(core, "a%d" % s)])
        return T.rq[:, W * s:W * s + W], T.rs[:, W * s:W * s + W]

    for group in [[s] for s in order[:N - 2]] + [order[N - 2:]]:
        held = [(s, part(s)) for s in group]
        for b in picks:
            if group[0] == r and b == picks[len(own)]:
                pe.wait_ge(sem.sx, got[(core, "sx")])
            for s, (q, p) in held:
                i = pe.matmul_mx(T.z[:, 512 * b:512 * b + W], T.sq[:, W * b:W * b + W], T.ss[:, W * b:W * b + W],
                                 q, p, s == r, s == order[-1])
                if s == order[-1]:
                    i.then_inc(sem["z%d" % b], 1)

    v.wait_ge(sem.ldw, 16)
    for b in picks:
        g.scalar.wait_ge(sem["z%d" % b], 1)
        g.scalar.activation(T.zc[:, W * b:W * b + W], T.z[:, 512 * b:512 * b + W], ActivationFunctionType.Identity,
                            scale=RATE).then_inc(sem["m%d" % b], 1)
        v.wait_ge(sem["m%d" % b], 1)
        v.tensor_tensor(T.ht[:, b:512:4], T.wt[:, b:512:4], T.zc[:, W * b:W * b + W],
                        AluOpType.subtract).then_inc(sem["r%d" % b], 1)
    for b in range(4):
        v.wait_ge(sem["r%d" % b], 1)
    v.quantize_mx(T.hq[:], T.hs[:], T.ht[:]).then_inc(sem.hqd, 1)
    v.wait_ge(sem.ldx, 16)
    v.quantize_mx(T.xq[:], T.xs[:], T.xt[:]).then_inc(sem.xqd, 1)

    for b in range(4):
        g.scalar.wait_ge(sem["r%d" % b], 1)
    g.scalar.wait_ge(sem.loc2, got[(core, "loc2")])
    g.scalar.dma_start(T.h[:], T.ht[:]).then_inc(sem.sth, 16)

    pe.wait_ge(sem.xqd, 1)
    for n, s in enumerate(Y_ORDER[r][:1] + [r] + Y_ORDER[r][1:]):
        if s == r:
            pe.wait_ge(sem.hqd, 1)
            q, p = T.hq[:], T.hs[:]
        else:
            for kind in "qs":
                pe.wait_ge(sem["c%s%d" % (kind, s)], got[(core, "c%s%d" % (kind, s))])
            q, p = T.cq[:, W * s:W * s + W], T.cs[:, W * s:W * s + W]
        bank = T.yp[:, 512 * n:512 * n + W] if n < 4 else T.z[:, 512 * (n - 4):512 * (n - 4) + W]
        pe.matmul_mx(bank, q, p, T.xq[:], T.xs[:], True, True).then_inc(sem["ym%d" % n], 1)
        v.wait_ge(sem["ym%d" % n], 1)
        v.tensor_copy(T.yt[:, W * s:W * s + W], bank).then_inc(sem["yc%d" % n], 1)
        g.sync.wait_ge(sem["yc%d" % n], 1)
        g.sync.dma_start(T.y[:, W * s:W * s + W], T.yt[:, W * s:W * s + W]).then_inc(sem.sty, 16)
    g.scalar.wait_ge(sem.sth, 16)
    g.sync.wait_ge(sem.sty, 16 * N)
